import numpy as np
import ml_dtypes


def mxq(x, axis, fmt="e4m3"):
    dtype, down = {"e4m3": (ml_dtypes.float8_e4m3fn, 7), "e5m2": (ml_dtypes.float8_e5m2, 14)}[fmt]
    v = np.moveaxis(np.asarray(x, np.float32).astype(ml_dtypes.bfloat16).astype(np.float64), axis, -1)
    blocks = v.reshape(v.shape[:-1] + (-1, 32))
    amax = np.abs(blocks).max(-1, keepdims=True)
    byte = np.maximum(np.where(amax > 0, np.frexp(amax)[1] - 1 + 127, 0) - down, 1)
    scale = np.exp2(byte - 127.0)
    codes = (blocks / scale).astype(np.float32).astype(dtype).astype(np.float64)
    return np.moveaxis((codes * scale).reshape(v.shape), -1, axis)


WIDE = False


def mx_kscale(k):
    if not WIDE:
        return np.ones(k)
    levels = np.array([10, -10, 5, -5, 0])
    if k % 512:
        return np.exp2(np.random.permutation(np.resize(levels, k // 32))).repeat(32)
    a = np.empty((k // 512, 16))
    for p in range(k // 512):
        a[p, :8] = np.random.permutation(np.resize(levels, 8))
        for g in range(8):
            far = levels[np.abs(levels - a[p, g]) >= 10]
            a[p, g + 8] = far[np.random.randint(len(far))]
    return np.exp2(a.ravel()).repeat(32)


def f64(x):
    return np.asarray(x).astype(np.float64)


def striped(idx):
    return np.tile(np.asarray(idx).reshape(-1, 16).T, (8, 1)).astype(np.uint16)


def unstriped(offs):
    return offs[:16].T.reshape(-1).astype(np.int64)


E2M1 = np.array([0.0, 0.5, 1.0, 1.5, 2.0, 3.0, 4.0, 6.0, -0.0, -0.5, -1.0, -1.5, -2.0, -3.0, -4.0, -6.0])


def pack_weight(w, fmt):
    k, n = w.shape
    w = f64(np.asarray(w, np.float32).astype(ml_dtypes.bfloat16)).reshape(k // 32, 32, n)
    amax = np.abs(w).max(1)
    if fmt == "e4m3":
        byte = np.frexp(amax)[1] - 1 + 127 - 7
    else:
        mant, ex = np.frexp(amax / 6.0)
        byte = np.where(mant > 0.5, ex, ex - 1) + 127
    byte = np.clip(np.where(amax > 0, byte, 1), 1, 254)
    scaled = (w * np.exp2(127.0 - byte)[:, None, :]).reshape(k, n).astype(np.float32)
    by_word = np.ascontiguousarray(scaled.reshape(k // 512, 128, 4, n).transpose(0, 1, 3, 2))
    if fmt == "e4m3":
        words = by_word.astype(ml_dtypes.float8_e4m3fn).view(np.uint8)
    else:
        c = by_word.astype(ml_dtypes.float4_e2m1fn).view(np.uint8) & 0xF
        words = (c[..., 0::2] | (c[..., 1::2] << 4)).reshape(k // 512, 128, 2 * n)
    return np.ascontiguousarray(words), np.ascontiguousarray(byte.astype(np.uint8).reshape(k // 512, 16, n))


def unpack_weight(words, scales, fmt):
    g, _, n = scales.shape
    words = np.ascontiguousarray(words).reshape(g, 128, n, -1)
    if fmt == "e4m3":
        vals = words.view(ml_dtypes.float8_e4m3fn).astype(np.float64)
    else:
        nib = np.empty((g, 128, n, 4), np.uint8)
        nib[..., 0::2] = words & 0xF
        nib[..., 1::2] = words >> 4
        vals = E2M1[nib]
    vals = vals * np.repeat(np.exp2(scales.astype(np.float64) - 127.0), 8, axis=1)[..., None]
    return vals.transpose(0, 1, 3, 2).reshape(g * 512, n)


D, E, T, I, Q = 512, 512, 1024, 256, 512


def setup_inputs():
    n = np.random.standard_normal
    idx = np.random.permutation(T)[:I]
    fd = mx_kscale(D)
    fq = mx_kscale(Q)
    keysp = pack_weight(n((D, T)) / fd[:, None], "e4m3")
    return {
        "query": (n((D, Q)) * 1.0 / np.sqrt(D) * fd[:, None]).astype(np.float32),
        "keys_words": keysp[0],
        "keys_scales": keysp[1],
        "aim": (np.random.uniform(0.5, 2.0, (Q, 1))).astype(np.float32),
        "soft": (np.random.uniform(0.5, 2.0, (Q, 1))).astype(np.float32),
        "qs": (np.random.uniform(2.0, 8.0, (Q, 1)) * fq[:, None]).astype(np.float32),
        "grows": (n((Q, E)) / fq[:, None]).astype(np.float32),
        "old": (n((E, T)) * 2.0).astype(np.float32),
        "fade": (np.random.uniform(0.5, 1.0, (1, T))).astype(np.float32),
        "offs": striped(idx),
    }


def reference(query, keys_words, keys_scales, aim, soft, qs, grows, old, fade, offs):
    idx = unstriped(offs)
    keysu = unpack_weight(keys_words, keys_scales, "e4m3")
    queryq = mxq(f64(query), 0, "e4m3")
    keysidxg = keysu[:, idx]
    a = queryq.T @ keysidxg
    p = 1.0 / (np.square(f64(aim) - a) + f64(soft))
    z = np.sum(p, axis=1, keepdims=True)
    w = p / z
    wq = w * f64(qs)
    growsq = mxq(f64(grows), 0, "e4m3")
    wqq = mxq(wq, 0, "e4m3")
    gv = growsq.T @ wqq
    gf = np.zeros((E, T))
    gf[:, idx] = gv
    y = f64(old) * f64(fade) + gf
    return y

@@ -1,0 +1,207 @@
+from contextlib import ExitStack
+
+import concourse.mybir as mybir
+from concourse.masks import make_identity
+
+D, E, T, I, Q = 512, 512, 1024, 256, 512
+FLOPS = 2 * D * Q * I + 2 * Q * E * I
+
+F32 = mybir.dt.float32
+BF16 = mybir.dt.bfloat16
+I32 = mybir.dt.int32
+U32 = mybir.dt.uint32
+U16 = mybir.dt.uint16
+U8 = mybir.dt.uint8
+FP8X4 = mybir.dt.float8_e4m3fn_x4
+ACT = mybir.ActivationFunctionType
+ALU = mybir.AluOpType
+
+P = 128
+PACK = 4
+BANK = 512
+
+
+def tile_attend_bnearpoint_v_kernel(tc, query, keys_words, keys_scales, aim, soft, qs, grows, old, fade, offs, out):
+    nc = tc.nc
+    with ExitStack() as ctx:
+        keep = ctx.enter_context(tc.tile_pool(name="keep", bufs=1))
+        psum = ctx.enter_context(tc.psum_pool(name="psum", bufs=1))
+
+        def sb(name, shape, dtype, tag=None):
+            return keep.tile(shape, dtype, name=name, tag=tag or name, align_bytes=64)
+
+        offsets = keep.tile([P, I // 16], U16, name="offsets")
+        nc.sync.dma_start(offsets[:], offs)
+
+        key_bytes = sb("key_bytes", [P, T], U8, "slot_c")
+        nc.gpsimd.memset(key_bytes[:].bitcast(I32), 0)
+        for quad in range(4):
+            nc.scalar.dma_start(
+                key_bytes[32 * quad : 32 * quad + 4, :].bitcast(I32),
+                keys_scales[0, 4 * quad : 4 * quad + 4, :].bitcast(I32),
+            )
+        one = sb("one", [P, 1], F32)
+        nc.gpsimd.memset(one[:], 1.0)
+        warm = sb("warm", [P, 1], F32, "slot_g")
+        nc.scalar.activation(warm[:], one[:], ACT.Abs_reciprocal_sqrt)
+
+        query_rows = query.rearrange("(p j) q -> p j q", j=PACK)
+        q_raw = []
+        for h in range(2):
+            t = sb(f"q_raw{h}", [P, PACK, Q // 2], F32, ("slot_a", "slot_b")[h])
+            nc.sync.dma_start(t[:], query_rows[:, :, h * (Q // 2) : (h + 1) * (Q // 2)])
+            q_raw.append(t)
+        key_words = sb("key_words", [P, T], U32, "slot_d")
+        nc.sync.dma_start(key_words[:].bitcast(I32), keys_words[0].rearrange("p n t -> p (n t)").bitcast(I32))
+        row_vec = {}
+        for name, vec in (("aim", aim), ("soft", soft), ("qs", qs)):
+            row_vec[name] = sb(name + "_sb", [P, PACK], F32)
+            nc.gpsimd.dma_start(row_vec[name][:], vec.rearrange("(p r) o -> p (r o)", r=PACK))
+        g_raw = sb("g_raw", [P, PACK, E], F32, "slot_g")
+        nc.sync.dma_start(g_raw[:], grows.rearrange("(p j) e -> p j e", j=PACK))
+
+        ident = sb("ident", [P, P], F32)
+        make_identity(nc, ident[:])
+        fade_rows = sb("fade_rows", [P, P], F32)
+        nc.gpsimd.memset(fade_rows[:], 0.0)
+        nc.sync.dma_start(fade_rows[0 : T // P, :], fade.rearrange("o (b p) -> (o b) p", p=P))
+
+        windows = []
+        for m in range(E // P):
+            w = sb(f"window{m}", [P, T], F32)
+            nc.vector.memset(w[:], 0.0)
+            windows.append(w)
+
+        kg_bytes = sb("kg_bytes", [P, I], U8)
+        nc.vector.tensor_copy(kg_bytes[:], key_bytes[:].indirect(offsets[:]))
+
+        q_codes = [sb(f"q_codes{r}", [P, P], U32) for r in range(PACK)]
+        q_scales = [sb(f"q_scales{r}", [P, P], U8) for r in range(PACK)]
+        for h in range(2):
+            src = q_raw[h][:].rearrange("p j (s r) -> p s j r", r=PACK)
+            q_bf = []
+            for a in range(2):
+                t = sb(f"q_bf{h}{a}", [P, 2, P // 2, PACK], BF16)
+                dst = t[:].rearrange("p r s j -> p s j r")
+                if a == 0:
+                    nc.vector.tensor_copy(dst, src[:, :, :, 0:2])
+                else:
+                    nc.scalar.copy(dst, src[:, :, :, 2:4])
+                q_bf.append(t)
+            cols = slice(h * (P // 2), (h + 1) * (P // 2))
+            for r in range(PACK):
+                nc.vector.quantize_mx(
+                    out=q_codes[r][:, cols].bitcast(FP8X4),
+                    scales=q_scales[r][:, cols],
+                    in_=q_bf[r // 2][:, r % 2, :, :].rearrange("p s j -> p (s j)"),
+                )
+
+        kg_words = sb("kg_words", [P, I], U32)
+        nc.vector.tensor_copy(kg_words[:], key_words[:].indirect(offsets[:]))
+
+        old_rows = old.rearrange("(m p) t -> p m t", p=P)
+        old_sb = {}
+        for h in range(2):
+            for pair in range(2):
+                t = sb(f"old{h}{pair}", [P, 2, BANK], F32, ("slot_a", "slot_b", "slot_c", "slot_d")[2 * h + pair])
+                nc.sync.dma_start(t[:], old_rows[:, 2 * pair : 2 * pair + 2, h * BANK : (h + 1) * BANK])
+                old_sb[h, pair] = t
+
+        score = []
+        for a in range(2):
+            bank = psum.tile([P, 2, I], F32, name=f"score{a}", tag="mm", bufs=2)
+            for k in range(2):
+                r = 2 * a + k
+                nc.tensor.matmul_mx(
+                    out=bank[:, k, :],
+                    lhsT=q_codes[r][:].bitcast(FP8X4),
+                    lhsT_scale=q_scales[r][:],
+                    rhs=kg_words[:].bitcast(FP8X4),
+                    rhs_scale=kg_bytes[:],
+                    start=True,
+                    stop=True,
+                )
+            score.append(bank)
+
+        g_codes = [sb(f"g_codes{a}", [P, 2 * P], U32) for a in range(2)]
+        g_scales = [sb(f"g_scales{a}", [P, 2 * P], U8) for a in range(2)]
+
+        def quantise_grows(a, tag):
+            g_bf = sb(f"g_bf{a}", [P, 2 * P, PACK], BF16, tag)
+            nc.vector.tensor_copy(
+                g_bf[:].rearrange("p (c i) j -> p c j i", i=4),
+                g_raw[:, :, 2 * a * P : 2 * (a + 1) * P].rearrange("p j (c i) -> p c j i", i=4),
+            )
+            nc.vector.quantize_mx(out=g_codes[a][:].bitcast(FP8X4), scales=g_scales[a][:], in_=g_bf[:].rearrange("p e j -> p (e j)"))
+
+        quantise_grows(0, "g_bf0")
+        w_bf = sb("w_bf", [P, I, PACK], BF16, "slot_w")
+        sq = [sb(f"sq{r}", [P, I], F32) for r in range(PACK)]
+        root = [sb(f"root{r}", [P, I], F32) for r in range(PACK)]
+        part = [sb(f"part{r}", [P, I], F32) for r in range(PACK)]
+        total = [sb(f"total{r}", [P, 1], F32) for r in range(PACK)]
+        inv = [sb(f"inv{r}", [P, 1], F32) for r in range(PACK)]
+
+        def square(r):
+            nc.scalar.activation(sq[r][:], score[r // 2][:, r % 2, :], ACT.Square, scale=-1.0, bias=row_vec["aim"][:, r : r + 1])
+
+        def inverse_root(r):
+            nc.scalar.activation(root[r][:], sq[r][:], ACT.Abs_reciprocal_sqrt, bias=row_vec["soft"][:, r : r + 1])
+
+        def parts(r):
+            nc.scalar.activation(part[r][:], root[r][:], ACT.Square, accum_out=total[r][:])
+            nc.vector.reciprocal(inv[r][:], total[r][:])
+            nc.vector.tensor_scalar(w_bf[:, :, r], part[r][:], inv[r][:], row_vec["qs"][:, r : r + 1], ALU.mult, ALU.mult)
+
+        for step in range(PACK + 2):
+            if step < PACK:
+                square(step)
+            if 1 <= step <= PACK:
+                inverse_root(step - 1)
+            if step >= 2:
+                parts(step - 2)
+        w_codes = sb("w_codes", [P, I], U32)
+        w_scales = sb("w_scales", [P, I], U8)
+        nc.vector.quantize_mx(out=w_codes[:].bitcast(FP8X4), scales=w_scales[:], in_=w_bf[:].rearrange("p i r -> p (i r)"))
+
+        for m in range(E // P):
+            if m == 1:
+                quantise_grows(1, "slot_w")
+            bank = psum.tile([P, I], F32, name=f"gv{m}", tag="mm", bufs=2)
+            cols = slice((m % 2) * P, (m % 2 + 1) * P)
+            nc.tensor.matmul_mx(
+                out=bank[:],
+                lhsT=g_codes[m // 2][:, cols].bitcast(FP8X4),
+                lhsT_scale=g_scales[m // 2][:, cols],
+                rhs=w_codes[:].bitcast(FP8X4),
+                rhs_scale=w_scales[:],
+                start=True,
+                stop=True,
+            )
+            gv = sb(f"gv_sb{m}", [P, I], F32)
+            nc.scalar.copy(gv[:], bank[:])
+            nc.vector.tensor_copy(windows[m][:].indirect(offsets[:]), gv[:])
+
+        fade_bank = psum.tile([P, PACK, P], F32, name="fade_bank", tag="turn", bufs=2)
+        nc.tensor.transpose(fade_bank[:, 0, :], fade_rows[:], ident[:])
+        fade_cols = sb("fade_cols", [P, T // P], F32)
+        nc.scalar.copy(fade_cols[:], fade_bank[:, 0, 0 : T // P])
+
+        for h in range(2):
+            faded = []
+            for b in range(4):
+                turned = psum.tile([P, PACK, P], F32, name=f"turned{h}{b}", tag="turn", bufs=2)
+                for m in range(E // P):
+                    nc.tensor.transpose(turned[:, m, :], old_sb[h, m // 2][:, m % 2, b * P : (b + 1) * P], ident[:])
+                f = sb(f"faded{h}{b}", [P, PACK, P], F32)
+                nc.scalar.activation(f[:], turned[:], ACT.Copy, scale=fade_cols[:, 4 * h + b : 4 * h + b + 1])
+                faded.append(f)
+            for m in range(E // P):
+                back = psum.tile([P, PACK, P], F32, name=f"back{h}{m}", tag="back", bufs=4)
+                for b in range(4):
+                    nc.tensor.transpose(back[:, b, :], faded[b][:, m, :], ident[:])
+                res = sb(f"res{h}{m}", [P, BANK], F32)
+                nc.vector.tensor_tensor(
+                    res[:], back[:].rearrange("p b t -> p (b t)"), windows[m][:, h * BANK : (h + 1) * BANK], ALU.add
+                )
+                nc.sync.dma_start(out[m * P : (m + 1) * P, h * BANK : (h + 1) * BANK], res[:])

@@ -30,33 +30,39 @@ def tile_attend_bnearpoint_v_kernel(tc, query, keys_words, keys_scales, aim, sof
         def sb(name, shape, dtype, tag=None):
             return keep.tile(shape, dtype, name=name, tag=tag or name, align_bytes=64)
 
+        def bank_tile(name, shape, bank):
+            return psum.tile(shape, F32, name=name, tag=f"bank{bank}")
+
         offsets = keep.tile([P, I // 16], U16, name="offsets")
         nc.sync.dma_start(offsets[:], offs)
 
         key_bytes = sb("key_bytes", [P, T], U8, "slot_c")
-        nc.gpsimd.memset(key_bytes[:].bitcast(I32), 0)
-        for quad in range(4):
-            nc.scalar.dma_start(
-                key_bytes[32 * quad : 32 * quad + 4, :].bitcast(I32),
-                keys_scales[0, 4 * quad : 4 * quad + 4, :].bitcast(I32),
-            )
-        one = sb("one", [P, 1], F32)
-        nc.gpsimd.memset(one[:], 1.0)
+        nc.vector.memset(key_bytes[:].bitcast(I32), 0)
+        one = sb("one", [P, 1], F32, "slot_v")
+        nc.vector.memset(one[:], 1.0)
         warm = sb("warm", [P, 1], F32, "slot_g")
         nc.scalar.activation(warm[:], one[:], ACT.Abs_reciprocal_sqrt)
 
-        query_rows = query.rearrange("(p j) q -> p j q", j=PACK)
-        q_raw = []
-        for h in range(2):
-            t = sb(f"q_raw{h}", [P, PACK, Q // 2], F32, ("slot_a", "slot_b")[h])
-            nc.sync.dma_start(t[:], query_rows[:, :, h * (Q // 2) : (h + 1) * (Q // 2)])
-            q_raw.append(t)
-        key_words = sb("key_words", [P, T], U32, "slot_d")
-        nc.sync.dma_start(key_words[:].bitcast(I32), keys_words[0].rearrange("p n t -> p (n t)").bitcast(I32))
         row_vec = {}
-        for name, vec in (("aim", aim), ("soft", soft), ("qs", qs)):
-            row_vec[name] = sb(name + "_sb", [P, PACK], F32)
-            nc.gpsimd.dma_start(row_vec[name][:], vec.rearrange("(p r) o -> p (r o)", r=PACK))
+
+        def load_rows(name, vec, tag):
+            row_vec[name] = sb(name + "_sb", [P, PACK], F32, tag)
+            nc.sync.dma_start(row_vec[name][:], vec.rearrange("(p r) o -> p (r o)", r=PACK))
+
+        query_rows = query.rearrange("(p j) q -> p j q", j=PACK)
+        q_raw = [sb(f"q_raw{h}", [P, PACK, Q // 2], F32, ("slot_a", "slot_b")[h]) for h in range(2)]
+        load_rows("aim", aim, None)
+        load_rows("soft", soft, None)
+        load_rows("qs", qs, None)
+        for h in range(2):
+            nc.sync.dma_start(q_raw[h][:], query_rows[:, :, h * (Q // 2) : (h + 1) * (Q // 2)])
+        for quad in range(4):
+            nc.sync.dma_start(
+                key_bytes[32 * quad : 32 * quad + 4, :].bitcast(I32),
+                keys_scales[0, 4 * quad : 4 * quad + 4, :].bitcast(I32),
+            )
+        key_words = sb("key_words", [P, T], U32, "slot_v")
+        nc.sync.dma_start(key_words[:].bitcast(I32), keys_words[0].rearrange("p n t -> p (n t)").bitcast(I32))
         g_raw = sb("g_raw", [P, PACK, E], F32, "slot_g")
         nc.sync.dma_start(g_raw[:], grows.rearrange("(p j) e -> p j e", j=PACK))
 
@@ -67,17 +73,19 @@ def tile_attend_bnearpoint_v_kernel(tc, query, keys_words, keys_scales, aim, sof
         nc.sync.dma_start(fade_rows[0 : T // P, :], fade.rearrange("o (b p) -> (o b) p", p=P))
 
         windows = []
-        for m in range(E // P):
-            w = sb(f"window{m}", [P, T], F32)
+
+        def zeroed_window(m, tag):
+            w = sb(f"window{m}", [P, T], F32, tag)
             nc.vector.memset(w[:], 0.0)
             windows.append(w)
 
-        kg_bytes = sb("kg_bytes", [P, I], U8)
-        nc.vector.tensor_copy(kg_bytes[:], key_bytes[:].indirect(offsets[:]))
+        for m in range(3):
+            zeroed_window(m, None)
 
         q_codes = [sb(f"q_codes{r}", [P, P], U32) for r in range(PACK)]
         q_scales = [sb(f"q_scales{r}", [P, P], U8) for r in range(PACK)]
-        for h in range(2):
+
+        def quantise_query(h):
             src = q_raw[h][:].rearrange("p j (s r) -> p s j r", r=PACK)
             q_bf = []
             for a in range(2):
@@ -96,20 +104,26 @@ def tile_attend_bnearpoint_v_kernel(tc, query, keys_words, keys_scales, aim, sof
                     in_=q_bf[r // 2][:, r % 2, :, :].rearrange("p s j -> p (s j)"),
                 )
 
+        quantise_query(0)
+        quantise_query(1)
+        kg_bytes = sb("kg_bytes", [P, I], U8)
+        nc.vector.tensor_copy(kg_bytes[:], key_bytes[:].indirect(offsets[:]))
+
         kg_words = sb("kg_words", [P, I], U32)
         nc.vector.tensor_copy(kg_words[:], key_words[:].indirect(offsets[:]))
+
 
         old_rows = old.rearrange("(m p) t -> p m t", p=P)
         old_sb = {}
         for h in range(2):
             for pair in range(2):
-                t = sb(f"old{h}{pair}", [P, 2, BANK], F32, ("slot_a", "slot_b", "slot_c", "slot_d")[2 * h + pair])
+                t = sb(f"old{h}{pair}", [P, 2, BANK], F32, ("slot_a", "slot_b", "slot_c", "q_bf11")[2 * h + pair])
                 nc.sync.dma_start(t[:], old_rows[:, 2 * pair : 2 * pair + 2, h * BANK : (h + 1) * BANK])
                 old_sb[h, pair] = t
 
         score = []
         for a in range(2):
-            bank = psum.tile([P, 2, I], F32, name=f"score{a}", tag="mm", bufs=2)
+            bank = bank_tile(f"score{a}", [P, 2, I], a)
             for k in range(2):
                 r = 2 * a + k
                 nc.tensor.matmul_mx(
@@ -123,6 +137,7 @@ def tile_attend_bnearpoint_v_kernel(tc, query, keys_words, keys_scales, aim, sof
                 )
             score.append(bank)
 
+        zeroed_window(3, "slot_v")
         g_codes = [sb(f"g_codes{a}", [P, 2 * P], U32) for a in range(2)]
         g_scales = [sb(f"g_scales{a}", [P, 2 * P], U8) for a in range(2)]
 
@@ -160,17 +175,20 @@ def tile_attend_bnearpoint_v_kernel(tc, query, keys_words, keys_scales, aim, sof
                 inverse_root(step - 1)
             if step >= 2:
                 parts(step - 2)
+        fade_bank = bank_tile("fade_bank", [P, P], 0)
+        nc.tensor.transpose(fade_bank[:], fade_rows[:], ident[:])
+        fade_cols = sb("fade_cols", [P, T // P], F32)
+        nc.scalar.copy(fade_cols[:], fade_bank[:, 0 : T // P])
         w_codes = sb("w_codes", [P, I], U32)
         w_scales = sb("w_scales", [P, I], U8)
         nc.vector.quantize_mx(out=w_codes[:].bitcast(FP8X4), scales=w_scales[:], in_=w_bf[:].rearrange("p i r -> p (i r)"))
 
-        for m in range(E // P):
-            if m == 1:
-                quantise_grows(1, "slot_w")
-            bank = psum.tile([P, I], F32, name=f"gv{m}", tag="mm", bufs=2)
+
+        def place(m, bank):
+            sums = bank_tile(f"gv{m}", [P, I], bank)
             cols = slice((m % 2) * P, (m % 2 + 1) * P)
             nc.tensor.matmul_mx(
-                out=bank[:],
+                out=sums[:],
                 lhsT=g_codes[m // 2][:, cols].bitcast(FP8X4),
                 lhsT_scale=g_scales[m // 2][:, cols],
                 rhs=w_codes[:].bitcast(FP8X4),
@@ -179,29 +197,51 @@ def tile_attend_bnearpoint_v_kernel(tc, query, keys_words, keys_scales, aim, sof
                 stop=True,
             )
             gv = sb(f"gv_sb{m}", [P, I], F32)
-            nc.scalar.copy(gv[:], bank[:])
+            nc.scalar.copy(gv[:], sums[:])
             nc.vector.tensor_copy(windows[m][:].indirect(offsets[:]), gv[:])
 
-        fade_bank = psum.tile([P, PACK, P], F32, name="fade_bank", tag="turn", bufs=2)
-        nc.tensor.transpose(fade_bank[:, 0, :], fade_rows[:], ident[:])
-        fade_cols = sb("fade_cols", [P, T // P], F32)
-        nc.scalar.copy(fade_cols[:], fade_bank[:, 0, 0 : T // P])
+        faded = {}
 
-        for h in range(2):
-            faded = []
-            for b in range(4):
-                turned = psum.tile([P, PACK, P], F32, name=f"turned{h}{b}", tag="turn", bufs=2)
-                for m in range(E // P):
-                    nc.tensor.transpose(turned[:, m, :], old_sb[h, m // 2][:, m % 2, b * P : (b + 1) * P], ident[:])
-                f = sb(f"faded{h}{b}", [P, PACK, P], F32)
-                nc.scalar.activation(f[:], turned[:], ACT.Copy, scale=fade_cols[:, 4 * h + b : 4 * h + b + 1])
-                faded.append(f)
+        def fade_block(h, b, bank):
+            turned = bank_tile(f"turned{h}{b}", [P, PACK, P], bank)
             for m in range(E // P):
-                back = psum.tile([P, PACK, P], F32, name=f"back{h}{m}", tag="back", bufs=4)
-                for b in range(4):
-                    nc.tensor.transpose(back[:, b, :], faded[b][:, m, :], ident[:])
-                res = sb(f"res{h}{m}", [P, BANK], F32)
-                nc.vector.tensor_tensor(
-                    res[:], back[:].rearrange("p b t -> p (b t)"), windows[m][:, h * BANK : (h + 1) * BANK], ALU.add
-                )
-                nc.sync.dma_start(out[m * P : (m + 1) * P, h * BANK : (h + 1) * BANK], res[:])
+                nc.tensor.transpose(turned[:, m, :], old_sb[h, m // 2][:, m % 2, b * P : (b + 1) * P], ident[:])
+            faded[h, b] = sb(f"faded{h}{b}", [P, PACK, P], F32)
+            nc.scalar.activation(faded[h, b][:], turned[:], ACT.Copy, scale=fade_cols[:, 4 * h + b : 4 * h + b + 1])
+
+        def finish(h, m, bank, on_gpsimd):
+            back = bank_tile(f"back{h}{m}", [P, PACK, P], bank)
+            for b in range(4):
+                nc.tensor.transpose(back[:, b, :], faded[h, b][:, m, :], ident[:])
+            kept = back[:].rearrange("p b t -> p (b t)")
+            res = sb(f"res{h}{m}", [P, BANK], F32)
+            placed = windows[m][:, h * BANK : (h + 1) * BANK]
+            if on_gpsimd:
+                staged = sb(f"staged{h}{m}", [P, BANK], F32)
+                nc.scalar.copy(staged[:], kept)
+                nc.gpsimd.tensor_tensor(res[:], staged[:], placed, ALU.add)
+            else:
+                nc.vector.tensor_tensor(res[:], kept, placed, ALU.add)
+            nc.sync.dma_start(out[m * P : (m + 1) * P, h * BANK : (h + 1) * BANK], res[:])
+
+        fade_block(0, 0, 2)
+        place(0, 2)
+        quantise_grows(1, "slot_w")
+        fade_block(0, 1, 3)
+        fade_block(0, 2, 4)
+        fade_block(0, 3, 5)
+        place(1, 1)
+        finish(0, 0, 4, False)
+        place(2, 0)
+        fade_block(1, 0, 6)
+        fade_block(1, 1, 7)
+        finish(0, 1, 5, False)
+        place(3, 1)
+        fade_block(1, 2, 3)
+        fade_block(1, 3, 2)
+        finish(0, 2, 6, False)
+        finish(1, 0, 7, False)
+        finish(1, 1, 3, False)
+        finish(0, 3, 4, False)
+        finish(1, 2, 5, False)
+        finish(1, 3, 2, False)

@@ -61,16 +61,22 @@ def tile_attend_bnearpoint_v_kernel(tc, query, keys_words, keys_scales, aim, sof
                 key_bytes[32 * quad : 32 * quad + 4, :].bitcast(I32),
                 keys_scales[0, 4 * quad : 4 * quad + 4, :].bitcast(I32),
             )
-        key_words = sb("key_words", [P, T], U32, "slot_v")
-        nc.sync.dma_start(key_words[:].bitcast(I32), keys_words[0].rearrange("p n t -> p (n t)").bitcast(I32))
-        g_raw = sb("g_raw", [P, PACK, E], F32, "slot_g")
-        nc.sync.dma_start(g_raw[:], grows.rearrange("(p j) e -> p j e", j=PACK))
-
         ident = sb("ident", [P, P], F32)
         make_identity(nc, ident[:])
         fade_rows = sb("fade_rows", [P, P], F32)
         nc.gpsimd.memset(fade_rows[:], 0.0)
         nc.sync.dma_start(fade_rows[0 : T // P, :], fade.rearrange("o (b p) -> (o b) p", p=P))
+
+        key_words = sb("key_words", [P, T], U32, "slot_v")
+        nc.sync.dma_start(key_words[:].bitcast(I32), keys_words[0].rearrange("p n t -> p (n t)").bitcast(I32))
+        old_rows = old.rearrange("(m p) t -> p m t", p=P)
+        old_sb = {}
+
+        def load_old(h, pair, tag):
+            old_sb[h, pair] = sb(f"old{h}{pair}", [P, 2, BANK], F32, tag)
+            nc.sync.dma_start(old_sb[h, pair][:], old_rows[:, 2 * pair : 2 * pair + 2, h * BANK : (h + 1) * BANK])
+
+        load_old(0, 0, "slot_g")
 
         windows = []
 
@@ -79,8 +85,16 @@ def tile_attend_bnearpoint_v_kernel(tc, query, keys_words, keys_scales, aim, sof
             nc.vector.memset(w[:], 0.0)
             windows.append(w)
 
-        for m in range(3):
+        for m in range(4):
             zeroed_window(m, None)
+
+        fade_bank = bank_tile("fade_bank", [P, P], 2)
+        nc.tensor.transpose(fade_bank[:], fade_rows[:], ident[:])
+        fade_cols = sb("fade_cols", [P, T // P], F32)
+        nc.scalar.copy(fade_cols[:], fade_bank[:, 0 : T // P])
+        fade_wide = bank_tile("fade_wide", [P, PACK, P], 3)
+        for b in range(4):
+            nc.tensor.transpose(fade_wide[:, b, :], fade_cols[:, b : b + 1].to_broadcast([P, P]), ident[:])
 
         q_codes = [sb(f"q_codes{r}", [P, P], U32) for r in range(PACK)]
         q_scales = [sb(f"q_scales{r}", [P, P], U8) for r in range(PACK)]
@@ -113,13 +127,11 @@ def tile_attend_bnearpoint_v_kernel(tc, query, keys_words, keys_scales, aim, sof
         nc.vector.tensor_copy(kg_words[:], key_words[:].indirect(offsets[:]))
 
 
-        old_rows = old.rearrange("(m p) t -> p m t", p=P)
-        old_sb = {}
-        for h in range(2):
-            for pair in range(2):
-                t = sb(f"old{h}{pair}", [P, 2, BANK], F32, ("slot_a", "slot_b", "slot_c", "q_bf11")[2 * h + pair])
-                nc.sync.dma_start(t[:], old_rows[:, 2 * pair : 2 * pair + 2, h * BANK : (h + 1) * BANK])
-                old_sb[h, pair] = t
+        g_raw = sb("g_raw", [P, PACK, E], F32, "slot_a")
+        nc.sync.dma_start(g_raw[:], grows.rearrange("(p j) e -> p j e", j=PACK))
+        load_old(1, 0, "slot_b")
+        load_old(1, 1, "q_bf11")
+        load_old(0, 1, "slot_c")
 
         score = []
         for a in range(2):
@@ -137,19 +149,19 @@ def tile_attend_bnearpoint_v_kernel(tc, query, keys_words, keys_scales, aim, sof
                 )
             score.append(bank)
 
-        zeroed_window(3, "slot_v")
-        g_codes = [sb(f"g_codes{a}", [P, 2 * P], U32) for a in range(2)]
-        g_scales = [sb(f"g_scales{a}", [P, 2 * P], U8) for a in range(2)]
+        g_codes = sb("g_codes", [P, E], U32)
+        g_scales = sb("g_scales", [P, E], U8)
 
-        def quantise_grows(a, tag):
-            g_bf = sb(f"g_bf{a}", [P, 2 * P, PACK], BF16, tag)
-            nc.vector.tensor_copy(
+        def quantise_grows(first, count, copy, tag):
+            cols = slice(first * P, (first + count) * P)
+            g_bf = sb(f"g_bf{first}", [P, count * P, PACK], BF16, tag)
+            copy(
                 g_bf[:].rearrange("p (c i) j -> p c j i", i=4),
-                g_raw[:, :, 2 * a * P : 2 * (a + 1) * P].rearrange("p j (c i) -> p c j i", i=4),
+                g_raw[:, :, cols].rearrange("p j (c i) -> p c j i", i=4),
             )
-            nc.vector.quantize_mx(out=g_codes[a][:].bitcast(FP8X4), scales=g_scales[a][:], in_=g_bf[:].rearrange("p e j -> p (e j)"))
+            nc.vector.quantize_mx(out=g_codes[:, cols].bitcast(FP8X4), scales=g_scales[:, cols], in_=g_bf[:].rearrange("p e j -> p (e j)"))
 
-        quantise_grows(0, "g_bf0")
+        quantise_grows(0, 1, nc.vector.tensor_copy, None)
         w_bf = sb("w_bf", [P, I, PACK], BF16, "slot_w")
         sq = [sb(f"sq{r}", [P, I], F32) for r in range(PACK)]
         root = [sb(f"root{r}", [P, I], F32) for r in range(PACK)]
@@ -175,10 +187,6 @@ def tile_attend_bnearpoint_v_kernel(tc, query, keys_words, keys_scales, aim, sof
                 inverse_root(step - 1)
             if step >= 2:
                 parts(step - 2)
-        fade_bank = bank_tile("fade_bank", [P, P], 0)
-        nc.tensor.transpose(fade_bank[:], fade_rows[:], ident[:])
-        fade_cols = sb("fade_cols", [P, T // P], F32)
-        nc.scalar.copy(fade_cols[:], fade_bank[:, 0 : T // P])
         w_codes = sb("w_codes", [P, I], U32)
         w_scales = sb("w_scales", [P, I], U8)
         nc.vector.quantize_mx(out=w_codes[:].bitcast(FP8X4), scales=w_scales[:], in_=w_bf[:].rearrange("p i r -> p (i r)"))
@@ -186,11 +194,11 @@ def tile_attend_bnearpoint_v_kernel(tc, query, keys_words, keys_scales, aim, sof
 
         def place(m, bank):
             sums = bank_tile(f"gv{m}", [P, I], bank)
-            cols = slice((m % 2) * P, (m % 2 + 1) * P)
+            cols = slice(m * P, (m + 1) * P)
             nc.tensor.matmul_mx(
                 out=sums[:],
-                lhsT=g_codes[m // 2][:, cols].bitcast(FP8X4),
-                lhsT_scale=g_scales[m // 2][:, cols],
+                lhsT=g_codes[:, cols].bitcast(FP8X4),
+                lhsT_scale=g_scales[:, cols],
                 rhs=w_codes[:].bitcast(FP8X4),
                 rhs_scale=w_scales[:],
                 start=True,
@@ -200,48 +208,66 @@ def tile_attend_bnearpoint_v_kernel(tc, query, keys_words, keys_scales, aim, sof
             nc.scalar.copy(gv[:], sums[:])
             nc.vector.tensor_copy(windows[m][:].indirect(offsets[:]), gv[:])
 
+        def store(h, m, res):
+            nc.sync.dma_start(out[m * P : (m + 1) * P, h * BANK : (h + 1) * BANK], res[:])
+
+        kept_low = {}
+
+        def fade_low(m, tag):
+            kept_low[m] = sb(f"kept_low{m}", [P, BANK], F32, tag)
+            nc.vector.tensor_tensor(
+                kept_low[m][:], fade_wide[:].rearrange("p b t -> p (b t)"), old_sb[0, m // 2][:, m % 2, :], ALU.mult
+            )
+
+        def finish_low(m, tag):
+            res = sb(f"res0{m}", [P, BANK], F32, tag)
+            nc.gpsimd.tensor_tensor(res[:], kept_low[m][:], windows[m][:, 0:BANK], ALU.add)
+            store(0, m, res)
+
         faded = {}
 
-        def fade_block(h, b, bank):
-            turned = bank_tile(f"turned{h}{b}", [P, PACK, P], bank)
+        def fade_block(b, bank):
+            turned = bank_tile(f"turned{b}", [P, PACK, P], bank)
             for m in range(E // P):
-                nc.tensor.transpose(turned[:, m, :], old_sb[h, m // 2][:, m % 2, b * P : (b + 1) * P], ident[:])
-            faded[h, b] = sb(f"faded{h}{b}", [P, PACK, P], F32)
-            nc.scalar.activation(faded[h, b][:], turned[:], ACT.Copy, scale=fade_cols[:, 4 * h + b : 4 * h + b + 1])
+                nc.tensor.transpose(turned[:, m, :], old_sb[1, m // 2][:, m % 2, b * P : (b + 1) * P], ident[:])
+            faded[b] = sb(f"faded{b}", [P, PACK, P], F32)
+            nc.scalar.activation(faded[b][:], turned[:], ACT.Copy, scale=fade_cols[:, 4 + b : 4 + b + 1])
 
-        def finish(h, m, bank, on_gpsimd):
-            back = bank_tile(f"back{h}{m}", [P, PACK, P], bank)
+        def finish_high(m, bank, on_gpsimd):
+            back = bank_tile(f"back{m}", [P, PACK, P], bank)
             for b in range(4):
-                nc.tensor.transpose(back[:, b, :], faded[h, b][:, m, :], ident[:])
+                nc.tensor.transpose(back[:, b, :], faded[b][:, m, :], ident[:])
             kept = back[:].rearrange("p b t -> p (b t)")
-            res = sb(f"res{h}{m}", [P, BANK], F32)
-            placed = windows[m][:, h * BANK : (h + 1) * BANK]
+            res = sb(f"res1{m}", [P, BANK], F32)
+            placed = windows[m][:, BANK:T]
             if on_gpsimd:
-                staged = sb(f"staged{h}{m}", [P, BANK], F32)
+                staged = sb(f"staged{m}", [P, BANK], F32)
                 nc.scalar.copy(staged[:], kept)
                 nc.gpsimd.tensor_tensor(res[:], staged[:], placed, ALU.add)
             else:
                 nc.vector.tensor_tensor(res[:], kept, placed, ALU.add)
-            nc.sync.dma_start(out[m * P : (m + 1) * P, h * BANK : (h + 1) * BANK], res[:])
+            store(1, m, res)
 
-        fade_block(0, 0, 2)
-        place(0, 2)
-        quantise_grows(1, "slot_w")
-        fade_block(0, 1, 3)
-        fade_block(0, 2, 4)
-        fade_block(0, 3, 5)
-        place(1, 1)
-        finish(0, 0, 4, False)
+        place(0, 6)
+        quantise_grows(1, 1, nc.scalar.copy, "sq3")
+        place(1, 7)
+        quantise_grows(2, 1, nc.scalar.copy, "root3")
         place(2, 0)
-        fade_block(1, 0, 6)
-        fade_block(1, 1, 7)
-        finish(0, 1, 5, False)
+        quantise_grows(3, 1, nc.scalar.copy, "part3")
         place(3, 1)
-        fade_block(1, 2, 3)
-        fade_block(1, 3, 2)
-        finish(0, 2, 6, False)
-        finish(1, 0, 7, False)
-        finish(1, 1, 3, False)
-        finish(0, 3, 4, False)
-        finish(1, 2, 5, False)
-        finish(1, 3, 2, False)
+        fade_low(0, None)
+        fade_low(1, None)
+        fade_low(2, "slot_w")
+        fade_low(3, "gv_sb1")
+        fade_block(0, 6)
+        fade_block(1, 7)
+        fade_block(2, 0)
+        fade_block(3, 1)
+        finish_low(0, None)
+        finish_low(1, None)
+        finish_low(2, None)
+        finish_high(0, 2, True)
+        finish_high(1, 4, True)
+        finish_low(3, "staged1")
+        finish_high(2, 5, False)
+        finish_high(3, 6, False)

@@ -88,13 +88,15 @@ def tile_attend_bnearpoint_v_kernel(tc, query, keys_words, keys_scales, aim, sof
         for m in range(4):
             zeroed_window(m, None)
 
-        fade_bank = bank_tile("fade_bank", [P, P], 2)
+        fade_bank = bank_tile("fade_bank", [P, P], 4)
         nc.tensor.transpose(fade_bank[:], fade_rows[:], ident[:])
         fade_cols = sb("fade_cols", [P, T // P], F32)
         nc.scalar.copy(fade_cols[:], fade_bank[:, 0 : T // P])
-        fade_wide = bank_tile("fade_wide", [P, PACK, P], 3)
+        fade_wide = bank_tile("fade_wide", [P, PACK, P], 5)
         for b in range(4):
             nc.tensor.transpose(fade_wide[:, b, :], fade_cols[:, b : b + 1].to_broadcast([P, P]), ident[:])
+        fade_wide_sb = sb("fade_wide_sb", [P, BANK], F32)
+        nc.scalar.copy(fade_wide_sb[:], fade_wide[:].rearrange("p b t -> p (b t)"))
 
         q_codes = [sb(f"q_codes{r}", [P, P], U32) for r in range(PACK)]
         q_scales = [sb(f"q_scales{r}", [P, P], U8) for r in range(PACK)]
@@ -129,24 +131,22 @@ def tile_attend_bnearpoint_v_kernel(tc, query, keys_words, keys_scales, aim, sof
 
         g_raw = sb("g_raw", [P, PACK, E], F32, "slot_a")
         nc.sync.dma_start(g_raw[:], grows.rearrange("(p j) e -> p j e", j=PACK))
-        load_old(1, 0, "slot_b")
-        load_old(1, 1, "q_bf11")
-        load_old(0, 1, "slot_c")
+        load_old(0, 1, "slot_b")
+        load_old(1, 0, "q_bf11")
+        load_old(1, 1, "slot_c")
 
         score = []
-        for a in range(2):
-            bank = bank_tile(f"score{a}", [P, 2, I], a)
-            for k in range(2):
-                r = 2 * a + k
-                nc.tensor.matmul_mx(
-                    out=bank[:, k, :],
-                    lhsT=q_codes[r][:].bitcast(FP8X4),
-                    lhsT_scale=q_scales[r][:],
-                    rhs=kg_words[:].bitcast(FP8X4),
-                    rhs_scale=kg_bytes[:],
-                    start=True,
-                    stop=True,
-                )
+        for r in range(PACK):
+            bank = bank_tile(f"score{r}", [P, I], r)
+            nc.tensor.matmul_mx(
+                out=bank[:],
+                lhsT=q_codes[r][:].bitcast(FP8X4),
+                lhsT_scale=q_scales[r][:],
+                rhs=kg_words[:].bitcast(FP8X4),
+                rhs_scale=kg_bytes[:],
+                start=True,
+                stop=True,
+            )
             score.append(bank)
 
         g_codes = sb("g_codes", [P, E], U32)
@@ -161,7 +161,7 @@ def tile_attend_bnearpoint_v_kernel(tc, query, keys_words, keys_scales, aim, sof
             )
             nc.vector.quantize_mx(out=g_codes[:, cols].bitcast(FP8X4), scales=g_scales[:, cols], in_=g_bf[:].rearrange("p e j -> p (e j)"))
 
-        quantise_grows(0, 1, nc.vector.tensor_copy, None)
+        quantise_grows(0, 2, nc.vector.tensor_copy, None)
         w_bf = sb("w_bf", [P, I, PACK], BF16, "slot_w")
         sq = [sb(f"sq{r}", [P, I], F32) for r in range(PACK)]
         root = [sb(f"root{r}", [P, I], F32) for r in range(PACK)]
@@ -170,7 +170,7 @@ def tile_attend_bnearpoint_v_kernel(tc, query, keys_words, keys_scales, aim, sof
         inv = [sb(f"inv{r}", [P, 1], F32) for r in range(PACK)]
 
         def square(r):
-            nc.scalar.activation(sq[r][:], score[r // 2][:, r % 2, :], ACT.Square, scale=-1.0, bias=row_vec["aim"][:, r : r + 1])
+            nc.scalar.activation(sq[r][:], score[r][:], ACT.Square, scale=-1.0, bias=row_vec["aim"][:, r : r + 1])
 
         def inverse_root(r):
             nc.scalar.activation(root[r][:], sq[r][:], ACT.Abs_reciprocal_sqrt, bias=row_vec["soft"][:, r : r + 1])
@@ -192,7 +192,7 @@ def tile_attend_bnearpoint_v_kernel(tc, query, keys_words, keys_scales, aim, sof
         nc.vector.quantize_mx(out=w_codes[:].bitcast(FP8X4), scales=w_scales[:], in_=w_bf[:].rearrange("p i r -> p (i r)"))
 
 
-        def place(m, bank):
+        def place(m, bank, tag):
             sums = bank_tile(f"gv{m}", [P, I], bank)
             cols = slice(m * P, (m + 1) * P)
             nc.tensor.matmul_mx(
@@ -204,7 +204,7 @@ def tile_attend_bnearpoint_v_kernel(tc, query, keys_words, keys_scales, aim, sof
                 start=True,
                 stop=True,
             )
-            gv = sb(f"gv_sb{m}", [P, I], F32)
+            gv = sb(f"gv_sb{m}", [P, I], F32, tag)
             nc.scalar.copy(gv[:], sums[:])
             nc.vector.tensor_copy(windows[m][:].indirect(offsets[:]), gv[:])
 
@@ -219,9 +219,9 @@ def tile_attend_bnearpoint_v_kernel(tc, query, keys_words, keys_scales, aim, sof
                 kept_low[m][:], fade_wide[:].rearrange("p b t -> p (b t)"), old_sb[0, m // 2][:, m % 2, :], ALU.mult
             )
 
-        def finish_low(m, tag):
-            res = sb(f"res0{m}", [P, BANK], F32, tag)
-            nc.gpsimd.tensor_tensor(res[:], kept_low[m][:], windows[m][:, 0:BANK], ALU.add)
+        def finish_low(m, engine):
+            res = sb(f"res0{m}", [P, BANK], F32)
+            engine.tensor_tensor(res[:], kept_low[m][:], windows[m][:, 0:BANK], ALU.add)
             store(0, m, res)
 
         faded = {}
@@ -248,26 +248,25 @@ def tile_attend_bnearpoint_v_kernel(tc, query, keys_words, keys_scales, aim, sof
                 nc.vector.tensor_tensor(res[:], kept, placed, ALU.add)
             store(1, m, res)
 
-        place(0, 6)
-        quantise_grows(1, 1, nc.scalar.copy, "sq3")
-        place(1, 7)
-        quantise_grows(2, 1, nc.scalar.copy, "root3")
-        place(2, 0)
-        quantise_grows(3, 1, nc.scalar.copy, "part3")
-        place(3, 1)
+        place(0, 6, None)
+        quantise_grows(2, 2, nc.scalar.copy, "root3")
+        place(1, 7, None)
+        place(2, 0, None)
         fade_low(0, None)
         fade_low(1, None)
         fade_low(2, "slot_w")
-        fade_low(3, "gv_sb1")
+        kept_low[3] = sb("kept_low3", [P, BANK], F32, "root3")
+        nc.gpsimd.tensor_tensor(kept_low[3][:], fade_wide_sb[:], old_sb[0, 1][:, 1, :], ALU.mult)
         fade_block(0, 6)
         fade_block(1, 7)
         fade_block(2, 0)
-        fade_block(3, 1)
-        finish_low(0, None)
-        finish_low(1, None)
-        finish_low(2, None)
-        finish_high(0, 2, True)
-        finish_high(1, 4, True)
-        finish_low(3, "staged1")
-        finish_high(2, 5, False)
-        finish_high(3, 6, False)
+        fade_block(3, 6)
+        finish_low(0, nc.gpsimd)
+        finish_low(1, nc.gpsimd)
+        finish_low(2, nc.gpsimd)
+        finish_high(0, 2, False)
+        finish_high(2, 3, True)
+        finish_high(1, 4, False)
+        place(3, 1, "window0")
+        finish_high(3, 5, False)
+        finish_low(3, nc.vector)

@@ -18,7 +18,11 @@ ALU = mybir.AluOpType
 
 P = 128
 PACK = 4
-BANK = 512
+QUADRANT = 32
+HALF = T // 2
+BLOCKS = HALF // P
+E_TILES = E // P
+LOW, HIGH = 0, 1
 
 
 def tile_attend_bnearpoint_v_kernel(tc, query, keys_words, keys_scales, aim, soft, qs, grows, old, fade, offs, out):
@@ -27,38 +31,52 @@ def tile_attend_bnearpoint_v_kernel(tc, query, keys_words, keys_scales, aim, sof
         keep = ctx.enter_context(tc.tile_pool(name="keep", bufs=1))
         psum = ctx.enter_context(tc.psum_pool(name="psum", bufs=1))
 
-        def sb(name, shape, dtype, tag=None):
-            return keep.tile(shape, dtype, name=name, tag=tag or name, align_bytes=64)
+        def sb(name, shape, dtype, after=None):
+            return keep.tile(shape, dtype, name=name, tag=after or name, align_bytes=64)
 
         def bank_tile(name, shape, bank):
             return psum.tile(shape, F32, name=name, tag=f"bank{bank}")
 
+        def quantise(codes, scales, values):
+            nc.vector.quantize_mx(out=codes.bitcast(FP8X4), scales=scales, in_=values)
+
+        def product(sums, lhs_codes, lhs_scales, rhs_codes, rhs_scales):
+            nc.tensor.matmul_mx(
+                out=sums,
+                lhsT=lhs_codes.bitcast(FP8X4),
+                lhsT_scale=lhs_scales,
+                rhs=rhs_codes.bitcast(FP8X4),
+                rhs_scale=rhs_scales,
+                start=True,
+                stop=True,
+            )
+
         offsets = keep.tile([P, I // 16], U16, name="offsets")
         nc.sync.dma_start(offsets[:], offs)
 
-        key_bytes = sb("key_bytes", [P, T], U8, "slot_c")
+        key_bytes = sb("key_bytes", [P, T], U8)
         nc.vector.memset(key_bytes[:].bitcast(I32), 0)
-        one = sb("one", [P, 1], F32, "slot_v")
+
+        one = sb("one", [P, 1], F32)
         nc.vector.memset(one[:], 1.0)
-        warm = sb("warm", [P, 1], F32, "slot_g")
+        warm = sb("warm", [P, 1], F32)
         nc.scalar.activation(warm[:], one[:], ACT.Abs_reciprocal_sqrt)
 
         row_vec = {}
 
-        def load_rows(name, vec, tag):
-            row_vec[name] = sb(name + "_sb", [P, PACK], F32, tag)
+        def load_rows(name, vec, after=None):
+            row_vec[name] = sb(name + "_sb", [P, PACK], F32, after)
             nc.sync.dma_start(row_vec[name][:], vec.rearrange("(p r) o -> p (r o)", r=PACK))
 
         query_rows = query.rearrange("(p j) q -> p j q", j=PACK)
-        q_raw = [sb(f"q_raw{h}", [P, PACK, Q // 2], F32, ("slot_a", "slot_b")[h]) for h in range(2)]
-        load_rows("aim", aim, None)
-        load_rows("soft", soft, None)
-        load_rows("qs", qs, None)
-        for h in range(2):
-            nc.sync.dma_start(q_raw[h][:], query_rows[:, :, h * (Q // 2) : (h + 1) * (Q // 2)])
-        for quad in range(4):
+        q_raw = [sb(f"q_raw{c}", [P, PACK, Q // 2], F32) for c in range(2)]
+        load_rows("aim", aim)
+        load_rows("soft", soft)
+        for c in range(2):
+            nc.sync.dma_start(q_raw[c][:], query_rows[:, :, c * (Q // 2) : (c + 1) * (Q // 2)])
+        for quad in range(P // QUADRANT):
             nc.sync.dma_start(
-                key_bytes[32 * quad : 32 * quad + 4, :].bitcast(I32),
+                key_bytes[QUADRANT * quad : QUADRANT * quad + 4, :].bitcast(I32),
                 keys_scales[0, 4 * quad : 4 * quad + 4, :].bitcast(I32),
             )
         ident = sb("ident", [P, P], F32)
@@ -67,102 +85,70 @@ def tile_attend_bnearpoint_v_kernel(tc, query, keys_words, keys_scales, aim, sof
         nc.gpsimd.memset(fade_rows[:], 0.0)
         nc.sync.dma_start(fade_rows[0 : T // P, :], fade.rearrange("o (b p) -> (o b) p", p=P))
 
-        key_words = sb("key_words", [P, T], U32, "slot_v")
+        key_words = sb("key_words", [P, T], U32, after="one")
         nc.sync.dma_start(key_words[:].bitcast(I32), keys_words[0].rearrange("p n t -> p (n t)").bitcast(I32))
-        old_rows = old.rearrange("(m p) t -> p m t", p=P)
-        old_sb = {}
-
-        def load_old(h, pair, tag):
-            old_sb[h, pair] = sb(f"old{h}{pair}", [P, 2, BANK], F32, tag)
-            nc.sync.dma_start(old_sb[h, pair][:], old_rows[:, 2 * pair : 2 * pair + 2, h * BANK : (h + 1) * BANK])
-
-        load_old(0, 0, "slot_g")
+        g_raw = sb("g_raw", [P, PACK, E], F32, after="warm")
+        nc.sync.dma_start(g_raw[:], grows.rearrange("(p j) e -> p j e", j=PACK))
 
         windows = []
-
-        def zeroed_window(m, tag):
-            w = sb(f"window{m}", [P, T], F32, tag)
-            nc.vector.memset(w[:], 0.0)
-            windows.append(w)
-
-        for m in range(4):
-            zeroed_window(m, None)
+        for m in range(E_TILES):
+            windows.append(sb(f"window{m}", [P, T], F32))
+            nc.vector.memset(windows[m][:], 0.0)
 
         fade_bank = bank_tile("fade_bank", [P, P], 4)
         nc.tensor.transpose(fade_bank[:], fade_rows[:], ident[:])
         fade_cols = sb("fade_cols", [P, T // P], F32)
         nc.scalar.copy(fade_cols[:], fade_bank[:, 0 : T // P])
-        fade_wide = bank_tile("fade_wide", [P, PACK, P], 5)
-        for b in range(4):
+        fade_wide = bank_tile("fade_wide", [P, BLOCKS, P], 5)
+        for b in range(BLOCKS):
             nc.tensor.transpose(fade_wide[:, b, :], fade_cols[:, b : b + 1].to_broadcast([P, P]), ident[:])
-        fade_wide_sb = sb("fade_wide_sb", [P, BANK], F32)
+        fade_wide_sb = sb("fade_wide_sb", [P, HALF], F32)
         nc.scalar.copy(fade_wide_sb[:], fade_wide[:].rearrange("p b t -> p (b t)"))
 
         q_codes = [sb(f"q_codes{r}", [P, P], U32) for r in range(PACK)]
         q_scales = [sb(f"q_scales{r}", [P, P], U8) for r in range(PACK)]
-
-        def quantise_query(h):
-            src = q_raw[h][:].rearrange("p j (s r) -> p s j r", r=PACK)
+        for c in range(2):
+            dealt = q_raw[c][:].rearrange("p j (s r) -> p s j r", r=PACK)
             q_bf = []
-            for a in range(2):
-                t = sb(f"q_bf{h}{a}", [P, 2, P // 2, PACK], BF16)
-                dst = t[:].rearrange("p r s j -> p s j r")
-                if a == 0:
-                    nc.vector.tensor_copy(dst, src[:, :, :, 0:2])
-                else:
-                    nc.scalar.copy(dst, src[:, :, :, 2:4])
-                q_bf.append(t)
-            cols = slice(h * (P // 2), (h + 1) * (P // 2))
+            for pair, copy in enumerate((nc.vector.tensor_copy, nc.scalar.copy)):
+                q_bf.append(sb(f"q_bf{c}{pair}", [P, 2, P // 2, PACK], BF16))
+                copy(q_bf[pair][:].rearrange("p r s j -> p s j r"), dealt[:, :, :, 2 * pair : 2 * pair + 2])
+            cols = slice(c * (P // 2), (c + 1) * (P // 2))
             for r in range(PACK):
-                nc.vector.quantize_mx(
-                    out=q_codes[r][:, cols].bitcast(FP8X4),
-                    scales=q_scales[r][:, cols],
-                    in_=q_bf[r // 2][:, r % 2, :, :].rearrange("p s j -> p (s j)"),
-                )
+                quantise(q_codes[r][:, cols], q_scales[r][:, cols], q_bf[r // 2][:, r % 2, :, :].rearrange("p s j -> p (s j)"))
 
-        quantise_query(0)
-        quantise_query(1)
-        kg_bytes = sb("kg_bytes", [P, I], U8)
-        nc.vector.tensor_copy(kg_bytes[:], key_bytes[:].indirect(offsets[:]))
+        listed_bytes = sb("listed_bytes", [P, I], U8)
+        nc.vector.tensor_copy(listed_bytes[:], key_bytes[:].indirect(offsets[:]))
+        listed_words = sb("listed_words", [P, I], U32)
+        nc.vector.tensor_copy(listed_words[:], key_words[:].indirect(offsets[:]))
 
-        kg_words = sb("kg_words", [P, I], U32)
-        nc.vector.tensor_copy(kg_words[:], key_words[:].indirect(offsets[:]))
-
-
-        g_raw = sb("g_raw", [P, PACK, E], F32, "slot_a")
-        nc.sync.dma_start(g_raw[:], grows.rearrange("(p j) e -> p j e", j=PACK))
-        load_old(0, 1, "slot_b")
-        load_old(1, 0, "q_bf11")
-        load_old(1, 1, "slot_c")
+        load_rows("qs", qs, after="q_bf00")
+        old_rows = old.rearrange("(m p) t -> p m t", p=P)
+        old_sb = {}
+        for half, pair, after in ((LOW, 0, "q_raw0"), (LOW, 1, "q_raw1"), (HIGH, 0, "q_bf11"), (HIGH, 1, "key_bytes")):
+            old_sb[half, pair] = sb(f"old{half}{pair}", [P, 2, HALF], F32, after)
+            nc.sync.dma_start(old_sb[half, pair][:], old_rows[:, 2 * pair : 2 * pair + 2, half * HALF : (half + 1) * HALF])
 
         score = []
         for r in range(PACK):
-            bank = bank_tile(f"score{r}", [P, I], r)
-            nc.tensor.matmul_mx(
-                out=bank[:],
-                lhsT=q_codes[r][:].bitcast(FP8X4),
-                lhsT_scale=q_scales[r][:],
-                rhs=kg_words[:].bitcast(FP8X4),
-                rhs_scale=kg_bytes[:],
-                start=True,
-                stop=True,
-            )
-            score.append(bank)
+            score.append(bank_tile(f"score{r}", [P, I], r))
+            product(score[r][:], q_codes[r][:], q_scales[r][:], listed_words[:], listed_bytes[:])
 
         g_codes = sb("g_codes", [P, E], U32)
         g_scales = sb("g_scales", [P, E], U8)
 
-        def quantise_grows(first, count, copy, tag):
-            cols = slice(first * P, (first + count) * P)
-            g_bf = sb(f"g_bf{first}", [P, count * P, PACK], BF16, tag)
+        def quantise_grows(pair, copy, after=None):
+            cols = slice(2 * pair * P, 2 * (pair + 1) * P)
+            g_bf = sb(f"g_bf{pair}", [P, 2 * P, PACK], BF16, after)
             copy(
-                g_bf[:].rearrange("p (c i) j -> p c j i", i=4),
-                g_raw[:, :, cols].rearrange("p j (c i) -> p c j i", i=4),
+                g_bf[:].rearrange("p (c n) j -> p c j n", n=4),
+                g_raw[:, :, cols].rearrange("p j (c n) -> p c j n", n=4),
             )
-            nc.vector.quantize_mx(out=g_codes[:, cols].bitcast(FP8X4), scales=g_scales[:, cols], in_=g_bf[:].rearrange("p e j -> p (e j)"))
+            quantise(g_codes[:, cols], g_scales[:, cols], g_bf[:].rearrange("p e j -> p (e j)"))
 
-        quantise_grows(0, 2, nc.vector.tensor_copy, None)
-        w_bf = sb("w_bf", [P, I, PACK], BF16, "slot_w")
+        quantise_grows(0, nc.vector.tensor_copy)
+
+        w_bf = sb("w_bf", [P, I, PACK], BF16)
         sq = [sb(f"sq{r}", [P, I], F32) for r in range(PACK)]
         root = [sb(f"root{r}", [P, I], F32) for r in range(PACK)]
         part = [sb(f"part{r}", [P, I], F32) for r in range(PACK)]
@@ -175,7 +161,7 @@ def tile_attend_bnearpoint_v_kernel(tc, query, keys_words, keys_scales, aim, sof
         def inverse_root(r):
             nc.scalar.activation(root[r][:], sq[r][:], ACT.Abs_reciprocal_sqrt, bias=row_vec["soft"][:, r : r + 1])
 
-        def parts(r):
+        def weigh(r):
             nc.scalar.activation(part[r][:], root[r][:], ACT.Square, accum_out=total[r][:])
             nc.vector.reciprocal(inv[r][:], total[r][:])
             nc.vector.tensor_scalar(w_bf[:, :, r], part[r][:], inv[r][:], row_vec["qs"][:, r : r + 1], ALU.mult, ALU.mult)
@@ -186,87 +172,71 @@ def tile_attend_bnearpoint_v_kernel(tc, query, keys_words, keys_scales, aim, sof
             if 1 <= step <= PACK:
                 inverse_root(step - 1)
             if step >= 2:
-                parts(step - 2)
+                weigh(step - 2)
         w_codes = sb("w_codes", [P, I], U32)
         w_scales = sb("w_scales", [P, I], U8)
-        nc.vector.quantize_mx(out=w_codes[:].bitcast(FP8X4), scales=w_scales[:], in_=w_bf[:].rearrange("p i r -> p (i r)"))
+        quantise(w_codes[:], w_scales[:], w_bf[:].rearrange("p i r -> p (i r)"))
 
-
-        def place(m, bank, tag):
+        def scatter(m, bank, after=None):
             sums = bank_tile(f"gv{m}", [P, I], bank)
             cols = slice(m * P, (m + 1) * P)
-            nc.tensor.matmul_mx(
-                out=sums[:],
-                lhsT=g_codes[:, cols].bitcast(FP8X4),
-                lhsT_scale=g_scales[:, cols],
-                rhs=w_codes[:].bitcast(FP8X4),
-                rhs_scale=w_scales[:],
-                start=True,
-                stop=True,
-            )
-            gv = sb(f"gv_sb{m}", [P, I], F32, tag)
+            product(sums[:], g_codes[:, cols], g_scales[:, cols], w_codes[:], w_scales[:])
+            gv = sb(f"gv_sb{m}", [P, I], F32, after)
             nc.scalar.copy(gv[:], sums[:])
             nc.vector.tensor_copy(windows[m][:].indirect(offsets[:]), gv[:])
 
-        def store(h, m, res):
-            nc.sync.dma_start(out[m * P : (m + 1) * P, h * BANK : (h + 1) * BANK], res[:])
+        def add_and_store(half, m, engine, faded):
+            cols = slice(half * HALF, (half + 1) * HALF)
+            res = sb(f"res{half}{m}", [P, HALF], F32)
+            engine.tensor_tensor(res[:], faded, windows[m][:, cols], ALU.add)
+            nc.sync.dma_start(out[m * P : (m + 1) * P, cols], res[:])
 
-        kept_low = {}
+        faded_low = {}
 
-        def fade_low(m, tag):
-            kept_low[m] = sb(f"kept_low{m}", [P, BANK], F32, tag)
+        def fade_low_on_vector(m, after=None):
+            faded_low[m] = sb(f"faded_low{m}", [P, HALF], F32, after)[:]
             nc.vector.tensor_tensor(
-                kept_low[m][:], fade_wide[:].rearrange("p b t -> p (b t)"), old_sb[0, m // 2][:, m % 2, :], ALU.mult
+                faded_low[m], fade_wide[:].rearrange("p b t -> p (b t)"), old_sb[LOW, m // 2][:, m % 2, :], ALU.mult
             )
 
-        def finish_low(m, engine):
-            res = sb(f"res0{m}", [P, BANK], F32)
-            engine.tensor_tensor(res[:], kept_low[m][:], windows[m][:, 0:BANK], ALU.add)
-            store(0, m, res)
+        faded_turned = {}
 
-        faded = {}
+        def fade_high_block(b, bank):
+            turned = bank_tile(f"turned{b}", [P, E_TILES, P], bank)
+            for m in range(E_TILES):
+                nc.tensor.transpose(turned[:, m, :], old_sb[HIGH, m // 2][:, m % 2, b * P : (b + 1) * P], ident[:])
+            faded_turned[b] = sb(f"faded_turned{b}", [P, E_TILES, P], F32)
+            nc.scalar.activation(faded_turned[b][:], turned[:], ACT.Copy, scale=fade_cols[:, BLOCKS + b : BLOCKS + b + 1])
 
-        def fade_block(b, bank):
-            turned = bank_tile(f"turned{b}", [P, PACK, P], bank)
-            for m in range(E // P):
-                nc.tensor.transpose(turned[:, m, :], old_sb[1, m // 2][:, m % 2, b * P : (b + 1) * P], ident[:])
-            faded[b] = sb(f"faded{b}", [P, PACK, P], F32)
-            nc.scalar.activation(faded[b][:], turned[:], ACT.Copy, scale=fade_cols[:, 4 + b : 4 + b + 1])
+        def turn_back(m, bank):
+            back = bank_tile(f"back{m}", [P, BLOCKS, P], bank)
+            for b in range(BLOCKS):
+                nc.tensor.transpose(back[:, b, :], faded_turned[b][:, m, :], ident[:])
+            return back[:].rearrange("p b t -> p (b t)")
 
-        def finish_high(m, bank, on_gpsimd):
-            back = bank_tile(f"back{m}", [P, PACK, P], bank)
-            for b in range(4):
-                nc.tensor.transpose(back[:, b, :], faded[b][:, m, :], ident[:])
-            kept = back[:].rearrange("p b t -> p (b t)")
-            res = sb(f"res1{m}", [P, BANK], F32)
-            placed = windows[m][:, BANK:T]
-            if on_gpsimd:
-                staged = sb(f"staged{m}", [P, BANK], F32)
-                nc.scalar.copy(staged[:], kept)
-                nc.gpsimd.tensor_tensor(res[:], staged[:], placed, ALU.add)
-            else:
-                nc.vector.tensor_tensor(res[:], kept, placed, ALU.add)
-            store(1, m, res)
+        scatter(0, 6)
+        quantise_grows(1, nc.scalar.copy, after="root3")
+        scatter(1, 7)
+        scatter(2, 0)
 
-        place(0, 6, None)
-        quantise_grows(2, 2, nc.scalar.copy, "root3")
-        place(1, 7, None)
-        place(2, 0, None)
-        fade_low(0, None)
-        fade_low(1, None)
-        fade_low(2, "slot_w")
-        kept_low[3] = sb("kept_low3", [P, BANK], F32, "root3")
-        nc.gpsimd.tensor_tensor(kept_low[3][:], fade_wide_sb[:], old_sb[0, 1][:, 1, :], ALU.mult)
-        fade_block(0, 6)
-        fade_block(1, 7)
-        fade_block(2, 0)
-        fade_block(3, 6)
-        finish_low(0, nc.gpsimd)
-        finish_low(1, nc.gpsimd)
-        finish_low(2, nc.gpsimd)
-        finish_high(0, 2, False)
-        finish_high(2, 3, True)
-        finish_high(1, 4, False)
-        place(3, 1, "window0")
-        finish_high(3, 5, False)
-        finish_low(3, nc.vector)
+        fade_low_on_vector(0)
+        fade_low_on_vector(1, after="w_bf")
+        faded_pair = sb("faded_pair", [P, 2 * HALF], F32, after="root3")
+        for k in range(2):
+            faded_low[2 + k] = faded_pair[:, k * HALF : (k + 1) * HALF]
+            nc.gpsimd.tensor_tensor(faded_low[2 + k], fade_wide_sb[:], old_sb[LOW, 1][:, k, :], ALU.mult)
+
+        for b, bank in enumerate((6, 7, 0, 6)):
+            fade_high_block(b, bank)
+
+        for m in range(E_TILES - 1):
+            add_and_store(LOW, m, nc.gpsimd, faded_low[m])
+        add_and_store(HIGH, 0, nc.vector, turn_back(0, 2))
+        back_in_psum = turn_back(2, 3)
+        back_in_sbuf = sb("back_in_sbuf", [P, HALF], F32)
+        nc.scalar.copy(back_in_sbuf[:], back_in_psum)
+        add_and_store(HIGH, 2, nc.gpsimd, back_in_sbuf[:])
+        add_and_store(HIGH, 1, nc.vector, turn_back(1, 4))
+        scatter(3, 1, after="window0")
+        add_and_store(HIGH, 3, nc.vector, turn_back(3, 5))
+        add_and_store(LOW, 3, nc.vector, faded_low[3])

from contextlib import ExitStack

import concourse.mybir as mybir
from concourse.masks import make_identity

D, E, T, I, Q = 512, 512, 1024, 256, 512
FLOPS = 2 * D * Q * I + 2 * Q * E * I

F32 = mybir.dt.float32
BF16 = mybir.dt.bfloat16
I32 = mybir.dt.int32
U32 = mybir.dt.uint32
U16 = mybir.dt.uint16
U8 = mybir.dt.uint8
FP8X4 = mybir.dt.float8_e4m3fn_x4
ACT = mybir.ActivationFunctionType
ALU = mybir.AluOpType

P = 128
PACK = 4
QUADRANT = 32
HALF = T // 2
BLOCKS = HALF // P
E_TILES = E // P
LOW, HIGH = 0, 1


def tile_attend_bnearpoint_v_kernel(tc, query, keys_words, keys_scales, aim, soft, qs, grows, old, fade, offs, out):
    nc = tc.nc
    with ExitStack() as ctx:
        keep = ctx.enter_context(tc.tile_pool(name="keep", bufs=1))
        psum = ctx.enter_context(tc.psum_pool(name="psum", bufs=1))

        def sb(name, shape, dtype, after=None):
            return keep.tile(shape, dtype, name=name, tag=after or name, align_bytes=64)

        def bank_tile(name, shape, bank):
            return psum.tile(shape, F32, name=name, tag=f"bank{bank}")

        def quantise(codes, scales, values):
            nc.vector.quantize_mx(out=codes.bitcast(FP8X4), scales=scales, in_=values)

        def product(sums, lhs_codes, lhs_scales, rhs_codes, rhs_scales):
            nc.tensor.matmul_mx(
                out=sums,
                lhsT=lhs_codes.bitcast(FP8X4),
                lhsT_scale=lhs_scales,
                rhs=rhs_codes.bitcast(FP8X4),
                rhs_scale=rhs_scales,
                start=True,
                stop=True,
            )

        offsets = keep.tile([P, I // 16], U16, name="offsets")
        nc.sync.dma_start(offsets[:], offs)

        key_bytes = sb("key_bytes", [P, T], U8)
        nc.vector.memset(key_bytes[:].bitcast(I32), 0)

        one = sb("one", [P, 1], F32)
        nc.vector.memset(one[:], 1.0)
        warm = sb("warm", [P, 1], F32)
        nc.scalar.activation(warm[:], one[:], ACT.Abs_reciprocal_sqrt)

        row_vec = {}

        def load_rows(name, vec, after=None):
            row_vec[name] = sb(name + "_sb", [P, PACK], F32, after)
            nc.sync.dma_start(row_vec[name][:], vec.rearrange("(p r) o -> p (r o)", r=PACK))

        query_rows = query.rearrange("(p j) q -> p j q", j=PACK)
        q_raw = [sb(f"q_raw{c}", [P, PACK, Q // 2], F32) for c in range(2)]
        load_rows("aim", aim)
        load_rows("soft", soft)
        for c in range(2):
            nc.sync.dma_start(q_raw[c][:], query_rows[:, :, c * (Q // 2) : (c + 1) * (Q // 2)])
        for quad in range(P // QUADRANT):
            nc.sync.dma_start(
                key_bytes[QUADRANT * quad : QUADRANT * quad + 4, :].bitcast(I32),
                keys_scales[0, 4 * quad : 4 * quad + 4, :].bitcast(I32),
            )
        ident = sb("ident", [P, P], F32)
        make_identity(nc, ident[:])
        fade_rows = sb("fade_rows", [P, P], F32)
        nc.gpsimd.memset(fade_rows[:], 0.0)
        nc.sync.dma_start(fade_rows[0 : T // P, :], fade.rearrange("o (b p) -> (o b) p", p=P))

        key_words = sb("key_words", [P, T], U32, after="one")
        nc.sync.dma_start(key_words[:].bitcast(I32), keys_words[0].rearrange("p n t -> p (n t)").bitcast(I32))
        g_raw = sb("g_raw", [P, PACK, E], F32, after="warm")
        nc.sync.dma_start(g_raw[:], grows.rearrange("(p j) e -> p j e", j=PACK))

        windows = []
        for m in range(E_TILES):
            windows.append(sb(f"window{m}", [P, T], F32))
            nc.vector.memset(windows[m][:], 0.0)

        fade_bank = bank_tile("fade_bank", [P, P], 4)
        nc.tensor.transpose(fade_bank[:], fade_rows[:], ident[:])
        fade_cols = sb("fade_cols", [P, T // P], F32)
        nc.scalar.copy(fade_cols[:], fade_bank[:, 0 : T // P])
        fade_wide = bank_tile("fade_wide", [P, BLOCKS, P], 5)
        for b in range(BLOCKS):
            nc.tensor.transpose(fade_wide[:, b, :], fade_cols[:, b : b + 1].to_broadcast([P, P]), ident[:])
        fade_wide_sb = sb("fade_wide_sb", [P, HALF], F32)
        nc.scalar.copy(fade_wide_sb[:], fade_wide[:].rearrange("p b t -> p (b t)"))

        q_codes = [sb(f"q_codes{r}", [P, P], U32) for r in range(PACK)]
        q_scales = [sb(f"q_scales{r}", [P, P], U8) for r in range(PACK)]
        for c in range(2):
            dealt = q_raw[c][:].rearrange("p j (s r) -> p s j r", r=PACK)
            q_bf = []
            for pair, copy in enumerate((nc.vector.tensor_copy, nc.scalar.copy)):
                q_bf.append(sb(f"q_bf{c}{pair}", [P, 2, P // 2, PACK], BF16))
                copy(q_bf[pair][:].rearrange("p r s j -> p s j r"), dealt[:, :, :, 2 * pair : 2 * pair + 2])
            cols = slice(c * (P // 2), (c + 1) * (P // 2))
            for r in range(PACK):
                quantise(q_codes[r][:, cols], q_scales[r][:, cols], q_bf[r // 2][:, r % 2, :, :].rearrange("p s j -> p (s j)"))

        listed_bytes = sb("listed_bytes", [P, I], U8)
        nc.vector.tensor_copy(listed_bytes[:], key_bytes[:].indirect(offsets[:]))
        listed_words = sb("listed_words", [P, I], U32)
        nc.vector.tensor_copy(listed_words[:], key_words[:].indirect(offsets[:]))

        load_rows("qs", qs, after="q_bf00")
        old_rows = old.rearrange("(m p) t -> p m t", p=P)
        old_sb = {}
        for half, pair, after in ((LOW, 0, "q_raw0"), (LOW, 1, "q_raw1"), (HIGH, 0, "q_bf11"), (HIGH, 1, "key_bytes")):
            old_sb[half, pair] = sb(f"old{half}{pair}", [P, 2, HALF], F32, after)
            nc.sync.dma_start(old_sb[half, pair][:], old_rows[:, 2 * pair : 2 * pair + 2, half * HALF : (half + 1) * HALF])

        score = []
        for r in range(PACK):
            score.append(bank_tile(f"score{r}", [P, I], r))
            product(score[r][:], q_codes[r][:], q_scales[r][:], listed_words[:], listed_bytes[:])

        g_codes = sb("g_codes", [P, E], U32)
        g_scales = sb("g_scales", [P, E], U8)

        def quantise_grows(pair, copy, after=None):
            cols = slice(2 * pair * P, 2 * (pair + 1) * P)
            g_bf = sb(f"g_bf{pair}", [P, 2 * P, PACK], BF16, after)
            copy(
                g_bf[:].rearrange("p (c n) j -> p c j n", n=4),
                g_raw[:, :, cols].rearrange("p j (c n) -> p c j n", n=4),
            )
            quantise(g_codes[:, cols], g_scales[:, cols], g_bf[:].rearrange("p e j -> p (e j)"))

        quantise_grows(0, nc.vector.tensor_copy)

        w_bf = sb("w_bf", [P, I, PACK], BF16)
        sq = [sb(f"sq{r}", [P, I], F32) for r in range(PACK)]
        root = [sb(f"root{r}", [P, I], F32) for r in range(PACK)]
        part = [sb(f"part{r}", [P, I], F32) for r in range(PACK)]
        total = [sb(f"total{r}", [P, 1], F32) for r in range(PACK)]
        inv = [sb(f"inv{r}", [P, 1], F32) for r in range(PACK)]

        def square(r):
            nc.scalar.activation(sq[r][:], score[r][:], ACT.Square, scale=-1.0, bias=row_vec["aim"][:, r : r + 1])

        def inverse_root(r):
            nc.scalar.activation(root[r][:], sq[r][:], ACT.Abs_reciprocal_sqrt, bias=row_vec["soft"][:, r : r + 1])

        def weigh(r):
            nc.scalar.activation(part[r][:], root[r][:], ACT.Square, accum_out=total[r][:])
            nc.vector.reciprocal(inv[r][:], total[r][:])
            nc.vector.tensor_scalar(w_bf[:, :, r], part[r][:], inv[r][:], row_vec["qs"][:, r : r + 1], ALU.mult, ALU.mult)

        for step in range(PACK + 2):
            if step < PACK:
                square(step)
            if 1 <= step <= PACK:
                inverse_root(step - 1)
            if step >= 2:
                weigh(step - 2)
        w_codes = sb("w_codes", [P, I], U32)
        w_scales = sb("w_scales", [P, I], U8)
        quantise(w_codes[:], w_scales[:], w_bf[:].rearrange("p i r -> p (i r)"))

        def scatter(m, bank, after=None):
            sums = bank_tile(f"gv{m}", [P, I], bank)
            cols = slice(m * P, (m + 1) * P)
            product(sums[:], g_codes[:, cols], g_scales[:, cols], w_codes[:], w_scales[:])
            gv = sb(f"gv_sb{m}", [P, I], F32, after)
            nc.scalar.copy(gv[:], sums[:])
            nc.vector.tensor_copy(windows[m][:].indirect(offsets[:]), gv[:])

        def add_and_store(half, m, engine, faded):
            cols = slice(half * HALF, (half + 1) * HALF)
            res = sb(f"res{half}{m}", [P, HALF], F32)
            engine.tensor_tensor(res[:], faded, windows[m][:, cols], ALU.add)
            nc.sync.dma_start(out[m * P : (m + 1) * P, cols], res[:])

        faded_low = {}

        def fade_low_on_vector(m, after=None):
            faded_low[m] = sb(f"faded_low{m}", [P, HALF], F32, after)[:]
            nc.vector.tensor_tensor(
                faded_low[m], fade_wide[:].rearrange("p b t -> p (b t)"), old_sb[LOW, m // 2][:, m % 2, :], ALU.mult
            )

        faded_turned = {}

        def fade_high_block(b, bank):
            turned = bank_tile(f"turned{b}", [P, E_TILES, P], bank)
            for m in range(E_TILES):
                nc.tensor.transpose(turned[:, m, :], old_sb[HIGH, m // 2][:, m % 2, b * P : (b + 1) * P], ident[:])
            faded_turned[b] = sb(f"faded_turned{b}", [P, E_TILES, P], F32)
            nc.scalar.activation(faded_turned[b][:], turned[:], ACT.Copy, scale=fade_cols[:, BLOCKS + b : BLOCKS + b + 1])

        def turn_back(m, bank):
            back = bank_tile(f"back{m}", [P, BLOCKS, P], bank)
            for b in range(BLOCKS):
                nc.tensor.transpose(back[:, b, :], faded_turned[b][:, m, :], ident[:])
            return back[:].rearrange("p b t -> p (b t)")

        scatter(0, 6)
        quantise_grows(1, nc.scalar.copy, after="root3")
        scatter(1, 7)
        scatter(2, 0)

        fade_low_on_vector(0)
        fade_low_on_vector(1, after="w_bf")
        faded_pair = sb("faded_pair", [P, 2 * HALF], F32, after="root3")
        for k in range(2):
            faded_low[2 + k] = faded_pair[:, k * HALF : (k + 1) * HALF]
            nc.gpsimd.tensor_tensor(faded_low[2 + k], fade_wide_sb[:], old_sb[LOW, 1][:, k, :], ALU.mult)

        for b, bank in enumerate((6, 7, 0, 6)):
            fade_high_block(b, bank)

        for m in range(E_TILES - 1):
            add_and_store(LOW, m, nc.gpsimd, faded_low[m])
        add_and_store(HIGH, 0, nc.vector, turn_back(0, 2))
        back_in_psum = turn_back(2, 3)
        back_in_sbuf = sb("back_in_sbuf", [P, HALF], F32)
        nc.scalar.copy(back_in_sbuf[:], back_in_psum)
        add_and_store(HIGH, 2, nc.gpsimd, back_in_sbuf[:])
        add_and_store(HIGH, 1, nc.vector, turn_back(1, 4))
        scatter(3, 1, after="window0")
        add_and_store(HIGH, 3, nc.vector, turn_back(3, 5))
        add_and_store(LOW, 3, nc.vector, faded_low[3])
